import numpy as np
import ml_dtypes


def mxq(x, axis, fmt="e4m3"):
    dtype, down = {"e4m3": (ml_dtypes.float8_e4m3fn, 7), "e5m2": (ml_dtypes.float8_e5m2, 14)}[fmt]
    v = np.moveaxis(np.asarray(x, np.float32).astype(ml_dtypes.bfloat16).astype(np.float64), axis, -1)
    blocks = v.reshape(v.shape[:-1] + (-1, 32))
    amax = np.abs(blocks).max(-1, keepdims=True)
    byte = np.maximum(np.where(amax > 0, np.frexp(amax)[1] - 1 + 127, 0) - down, 1)
    scale = np.exp2(byte - 127.0)
    codes = (blocks / scale).astype(np.float32).astype(dtype).astype(np.float64)
    return np.moveaxis((codes * scale).reshape(v.shape), -1, axis)


WIDE = False


def mx_kscale(k):
    if not WIDE:
        return np.ones(k)
    levels = np.array([10, -10, 5, -5, 0])
    if k % 512:
        return np.exp2(np.random.permutation(np.resize(levels, k // 32))).repeat(32)
    a = np.empty((k // 512, 16))
    for p in range(k // 512):
        a[p, :8] = np.random.permutation(np.resize(levels, 8))
        for g in range(8):
            far = levels[np.abs(levels - a[p, g]) >= 10]
            a[p, g + 8] = far[np.random.randint(len(far))]
    return np.exp2(a.ravel()).repeat(32)


def f64(x):
    return np.asarray(x).astype(np.float64)


def striped(idx):
    return np.tile(idx.reshape(-1, 16).T, (8, 1)).astype(np.uint16)


def unstriped(offs):
    return offs[:16].T.reshape(-1).astype(np.int64)


def striped8(idx):
    return np.concatenate([x.reshape(-1, 16).T for x in idx]).astype(np.uint16)


def runs(offs, k):
    lists = np.stack([offs[16 * r : 16 * r + 16].T.reshape(-1) for r in range(8)]).astype(np.int64)
    return lists[np.arange(k) % 512 // 64]


def pack_weight(w):
    k, n = w.shape
    w = f64(np.asarray(w, np.float32).astype(ml_dtypes.bfloat16)).reshape(k // 32, 32, n)
    amax = np.abs(w).max(1)
    byte = np.clip(np.where(amax > 0, np.frexp(amax)[1] - 1 + 127 - 7, 1), 1, 254)
    scaled = (w * np.exp2(127.0 - byte)[:, None, :]).reshape(k, n).astype(np.float32)
    words = np.ascontiguousarray(scaled.reshape(k // 512, 128, 4, n).transpose(0, 1, 3, 2)).astype(ml_dtypes.float8_e4m3fn).view(np.uint8)
    return words, np.ascontiguousarray(byte.astype(np.uint8).reshape(k // 512, 16, n))


def unpack_weight(words, scales):
    g, p, n, _ = words.shape
    vals = np.ascontiguousarray(words).view(ml_dtypes.float8_e4m3fn).astype(np.float64) * np.repeat(np.exp2(scales.astype(np.float64) - 127.0), 8, axis=1)[..., None]
    return vals.transpose(0, 1, 3, 2).reshape(g * 512, n)


E2M1 = np.array([0.0, 0.5, 1.0, 1.5, 2.0, 3.0, 4.0, 6.0, -0.0, -0.5, -1.0, -1.5, -2.0, -3.0, -4.0, -6.0])


def pack_fp4(w):
    k, n = w.shape
    w = f64(np.asarray(w, np.float32).astype(ml_dtypes.bfloat16)).reshape(k // 32, 32, n)
    amax = np.abs(w).max(1)
    mant, ex = np.frexp(amax / 6.0)
    byte = np.clip(np.where(amax > 0, np.where(mant > 0.5, ex, ex - 1) + 127, 1), 1, 254)
    scaled = (w * np.exp2(127.0 - byte)[:, None, :]).reshape(k, n).astype(np.float32)
    c = np.ascontiguousarray(scaled.reshape(k // 512, 128, 4, n).transpose(0, 1, 3, 2)).astype(ml_dtypes.float4_e2m1fn).view(np.uint8) & 0xF
    words = (c[..., 0::2] | (c[..., 1::2] << 4)).reshape(k // 512, 128, 2 * n)
    return np.ascontiguousarray(words), np.ascontiguousarray(byte.astype(np.uint8).reshape(k // 512, 16, n))


def unpack_fp4(words, scales):
    g, _, n = scales.shape
    words = np.ascontiguousarray(words).reshape(g, 128, n, 2)
    nib = np.empty((g, 128, n, 4), np.uint8)
    nib[..., 0::2] = words & 0xF
    nib[..., 1::2] = words >> 4
    vals = E2M1[nib] * np.repeat(np.exp2(scales.astype(np.float64) - 127.0), 8, axis=1)[..., None]
    return vals.transpose(0, 1, 3, 2).reshape(g * 512, n)


def planes(y):
    n, m = y.shape
    v = y.astype(np.float32).astype(ml_dtypes.bfloat16).astype(np.float64).reshape(n // 32, 32, m)
    top = np.abs(v).max(1)
    byte = np.clip(np.where(top > 0, np.frexp(top)[1] - 1 + 127 - 7, 1), 1, 254)
    codes = (v * np.exp2(127.0 - byte)[:, None, :]).reshape(n, m).astype(np.float32).astype(ml_dtypes.float8_e4m3fn).view(np.uint8)
    words = codes.reshape(n // 512, 128, 4, m).transpose(0, 1, 3, 2)
    return np.ascontiguousarray(words), np.ascontiguousarray(byte.astype(np.uint8).reshape(n // 512, 16, m))


K, T, S, N, H, U = 512, 2048, 256, 512, 512, 1024


def setup_inputs():
    n = np.random.standard_normal
    s = mx_kscale(K)[:, None]
    u = mx_kscale(H)
    packed_xT = pack_weight(n((K, T)) * s)
    packed_w1 = pack_fp4(n((K, H)) / np.sqrt(K) / s)
    packed_w2 = pack_fp4(n((K, H)) / np.sqrt(K) / s)
    packed_w3 = pack_fp4(n((H, N)) / np.sqrt(H) / u[:, None])
    return {
        "x_words": packed_xT[0],
        "x_scales": packed_xT[1],
        "w1_words": packed_w1[0],
        "w1_scales": packed_w1[1],
        "w2_words": packed_w2[0],
        "w2_scales": packed_w2[1],
        "gn": (np.random.uniform(0.5, 1.5, (H, 1)) * u[:, None]).astype(np.float32),
        "w3_words": packed_w3[0],
        "w3_scales": packed_w3[1],
        "mem": n((N, U)).astype(np.float32),
        "offs": striped(np.random.permutation(T)[:S]),
        "two": striped(np.random.permutation(T)[:S]),
        "n1": striped8(np.stack([np.random.permutation(S) for _ in range(8)])),
        "n2": striped8(np.stack([np.random.permutation(S) for _ in range(8)])),
        "n3": striped(np.random.permutation(U)[:S]),
    }


def reference(x_words, x_scales, w1_words, w1_scales, w2_words, w2_scales, gn, w3_words, w3_scales, mem, offs, two, n1, n2, n3):
    xq = unpack_weight(x_words, x_scales)[:, unstriped(offs)]
    y = unpack_fp4(w1_words, w1_scales).T @ xq
    x_two = unpack_weight(x_words, x_scales)[:, unstriped(two)]
    d = unpack_fp4(w2_words, w2_scales).T @ x_two
    z = f64(gn) * (y[np.arange(H)[:, None], runs(n1, H)] - (np.tanh(d) * (d[np.arange(H)[:, None], runs(n2, H)])))
    h = unpack_fp4(w3_words, w3_scales).T @ mxq(z, 0, "e4m3")
    nw = np.maximum(h, 0.5 * f64(mem)[:, unstriped(n3)])
    out = f64(mem).copy()
    out[:, unstriped(n3)] = nw
    return (out,) + planes(out)

@@ -1,0 +1,174 @@
+from contextlib import ExitStack
+
+import concourse.mybir as mybir
+
+K, T, S, N, H, U = 512, 2048, 256, 512, 512, 1024
+FLOPS = 3 * 2 * 512 * 512 * 256
+
+F32 = mybir.dt.float32
+BF16 = mybir.dt.bfloat16
+I32 = mybir.dt.int32
+U32 = mybir.dt.uint32
+U16 = mybir.dt.uint16
+U8 = mybir.dt.uint8
+FP8X4 = mybir.dt.float8_e4m3fn_x4
+FP4X4 = mybir.dt.float4_e2m1fn_x4
+ALU = mybir.AluOpType
+ACT = mybir.ActivationFunctionType
+
+P = 128
+PACK = 4
+HALF = S // 2
+CHUNKS = 4
+CW = U // CHUNKS
+
+
+def tile_picked_twlsoftbpagex_none_po_kernel(
+    tc, x_words, x_scales, w1_words, w1_scales, w2_words, w2_scales, gn, w3_words, w3_scales, mem,
+    offs, two, n1, n2, n3, out_0, out_1, out_2,
+):
+    nc = tc.nc
+    with ExitStack() as ctx:
+        sb = ctx.enter_context(tc.tile_pool(name="sb", bufs=1))
+        ps = ctx.enter_context(tc.psum_pool(name="ps", bufs=1))
+
+        def tile(name, shape, dtype):
+            return sb.tile(shape, dtype, name=name, align_bytes=64)
+
+        def load_list(name, src):
+            t = tile(name, [P, S // 16], U16)
+            nc.sync.dma_start(t[:], src)
+            return t
+
+        def load_scales(name, src, width, queue):
+            t = tile(name, [P, width], U8)
+            nc.vector.memset(t[:].bitcast(I32), 0)
+            for q in range(4):
+                queue.dma_start(t[32 * q : 32 * q + 4, :].bitcast(I32), src[0, 4 * q : 4 * q + 4, :].bitcast(I32))
+            return t
+
+        def load_words(name, src):
+            t = tile(name, [P, 2 * H], U8)
+            nc.sync.dma_start(t[:].bitcast(I32), src[0].bitcast(I32))
+            return t
+
+        def deal(name, words, scales):
+            dw = tile(name + "_dw", [P, 2 * H], U8)
+            ds = tile(name + "_ds", [P, H], U8)
+            nc.vector.tensor_copy(dw[:].rearrange("p (t m b) -> p t m b", t=PACK, b=2),
+                                  words[:].rearrange("p (m t b) -> p t m b", t=PACK, b=2))
+            nc.vector.tensor_copy(ds[:].rearrange("p (t m) -> p t m", t=PACK),
+                                  scales[:].rearrange("p (m t) -> p t m", t=PACK))
+            return dw, ds
+
+        def pick(name, xw, xs, lst):
+            gw = tile(name + "_w", [P, S], I32)
+            gs = tile(name + "_s", [P, S], U8)
+            nc.vector.tensor_copy(gw[:].bitcast(U32), xw[:].bitcast(U32).indirect(lst[:]))
+            nc.vector.tensor_copy(gs[:], xs[:].indirect(lst[:]))
+            return gw, gs
+
+        def product(out, w, t, rw, rs):
+            dw, ds = w
+            nc.tensor.matmul_mx(out=out, lhsT=dw[:, 2 * P * t : 2 * P * (t + 1)].bitcast(FP4X4),
+                                lhsT_scale=ds[:, P * t : P * (t + 1)], rhs=rw.bitcast(FP8X4), rhs_scale=rs,
+                                start=True, stop=True)
+
+        l_two = load_list("l_two", two)
+        w2w = load_words("w2w", w2_words)
+        l_offs = load_list("l_offs", offs)
+        w2s = load_scales("w2s", w2_scales, H, nc.sync)
+        xw = tile("xw", [P, T], I32)
+        nc.sync.dma_start(xw[:], x_words[0].rearrange("p c r -> p (c r)").bitcast(I32))
+        xs = load_scales("xs", x_scales, T, nc.sync)
+        w1w = load_words("w1w", w1_words)
+        w1s = load_scales("w1s", w1_scales, H, nc.sync)
+        gain = tile("gain", [P, PACK], F32)
+        nc.sync.dma_start(gain[:], gn.rearrange("(p t) o -> p (t o)", t=PACK))
+        l_n2 = load_list("l_n2", n2)
+        l_n1 = load_list("l_n1", n1)
+        w3w = load_words("w3w", w3_words)
+        w3s = load_scales("w3s", w3_scales, N, nc.sync)
+        l_n3 = load_list("l_n3", n3)
+        mem_rows = mem.rearrange("(p t) c -> p t c", t=PACK)
+        out_rows = out_0.rearrange("(p t) c -> p t c", t=PACK)
+        page = []
+        for t in range(PACK):
+            pg = tile(f"page{t}", [P, U], F32)
+            nc.sync.dma_start(pg[:], mem_rows[:, t, :])
+            page.append(pg)
+
+        w2 = deal("w2", w2w, w2s)
+        w1 = deal("w1", w1w, w1s)
+        tw, ts = pick("two", xw, xs, l_two)
+        ow, osc = pick("offs", xw, xs, l_offs)
+
+        d_ps = [ps.tile([P, S], F32, name=f"d_ps{t}") for t in range(PACK)]
+        y_ps = [ps.tile([P, 2, S], F32, name=f"y_ps{i}") for i in range(2)]
+        for t in range(PACK):
+            product(d_ps[t][:], w2, t, tw[:], ts[:])
+        for t in range(PACK):
+            product(y_ps[t // 2][:, t % 2, :], w1, t, ow[:], osc[:])
+
+        th = tile("th", [P, PACK, S], F32)
+        dwin, ywin = [], []
+        for t in range(PACK):
+            nc.scalar.activation(th[:, t, :], d_ps[t][:], ACT.Tanh)
+            dw = tile(f"dwin{t}", [P, S], F32)
+            nc.vector.tensor_scalar(dw[:], d_ps[t][:], gain[:, t : t + 1], None, ALU.mult)
+            dwin.append(dw)
+        for t in range(PACK):
+            yw = tile(f"ywin{t}", [P, S], F32)
+            nc.vector.tensor_scalar(yw[:], y_ps[t // 2][:, t % 2, :], gain[:, t : t + 1], None, ALU.mult)
+            ywin.append(yw)
+        w3 = deal("w3", w3w, w3s)
+
+        h_ps = []
+        for a in range(2):
+            cols = slice(a * HALF // 16, (a + 1) * HALF // 16)
+            dg = tile(f"dg{a}", [P, PACK, HALF], F32)
+            yg = tile(f"yg{a}", [P, PACK, HALF], F32)
+            for t in range(PACK):
+                nc.scalar.activation(dg[:, t, :], dwin[t][:].indirect(l_n2[:, cols]), ACT.Copy)
+            for t in range(PACK):
+                nc.scalar.activation(yg[:, t, :], ywin[t][:].indirect(l_n1[:, cols]), ACT.Copy)
+            q = tile(f"q{a}", [P, PACK, HALF], F32)
+            nc.vector.tensor_tensor(q[:], dg[:], th[:, :, a * HALF : (a + 1) * HALF], ALU.mult)
+            z = tile(f"z{a}", [P, HALF * PACK], BF16)
+            nc.vector.tensor_tensor(z[:].rearrange("p (c i t) -> p c t i", i=4, t=PACK),
+                                    yg[:].rearrange("p t (c i) -> p c t i", i=4),
+                                    q[:].rearrange("p t (c i) -> p c t i", i=4), ALU.subtract)
+            zw = tile(f"zw{a}", [P, HALF], I32)
+            zs = tile(f"zs{a}", [P, HALF], U8)
+            nc.vector.quantize_mx(out=zw[:].bitcast(FP8X4), scales=zs[:], in_=z[:])
+            hp = ps.tile([P, PACK, HALF], F32, name=f"h_ps{a}")
+            for t in range(PACK):
+                product(hp[:, t, :], w3, t, zw[:], zs[:])
+            h_ps.append(hp)
+
+        old = tile("old", [P, PACK, S], F32)
+        for t in range(PACK):
+            nc.scalar.activation(old[:, t, :], page[t][:].indirect(l_n3[:]), ACT.Copy)
+        new = tile("new", [P, PACK, S], F32)
+        for a in range(2):
+            cols = slice(a * HALF, (a + 1) * HALF)
+            nc.vector.scalar_tensor_tensor(new[:, :, cols], old[:, :, cols], 0.5, h_ps[a][:], ALU.mult, ALU.max)
+
+        rounded = [tile(f"rounded{c}", [P, CW, PACK], BF16) for c in range(CHUNKS)]
+        codes = [tile(f"codes{c}", [P, CW], I32) for c in range(CHUNKS)]
+        plane = tile("plane", [P, U], U8)
+        words_out = out_1[0].rearrange("p c r -> p (c r)").bitcast(I32)
+        for t in range(PACK):
+            nc.scalar.activation(page[t][:].indirect(l_n3[:]), new[:, t, :], ACT.Copy)
+            nc.sync.dma_start(out_rows[:, t, :], page[t][:])
+            for c in range(CHUNKS):
+                cols = slice(c * CW, (c + 1) * CW)
+                nc.vector.tensor_copy(rounded[c][:, :, t], page[t][:, cols])
+        for c in range(CHUNKS):
+            cols = slice(c * CW, (c + 1) * CW)
+            nc.vector.quantize_mx(out=codes[c][:].bitcast(FP8X4), scales=plane[:, cols],
+                                  in_=rounded[c][:].rearrange("p c t -> p (c t)"))
+            nc.sync.dma_start(words_out[:, cols], codes[c][:])
+        for q in range(4):
+            queue = nc.scalar if q % 2 else nc.sync
+            queue.dma_start(out_2[0, 4 * q : 4 * q + 4, :].bitcast(I32), plane[32 * q : 32 * q + 4, :].bitcast(I32))

@@ -18,7 +18,6 @@ ACT = mybir.ActivationFunctionType
 
 P = 128
 PACK = 4
-HALF = S // 2
 CHUNKS = 4
 CW = U // CHUNKS
 
@@ -32,19 +31,19 @@ def tile_picked_twlsoftbpagex_none_po_kernel(
         sb = ctx.enter_context(tc.tile_pool(name="sb", bufs=1))
         ps = ctx.enter_context(tc.psum_pool(name="ps", bufs=1))
 
-        def tile(name, shape, dtype):
-            return sb.tile(shape, dtype, name=name, align_bytes=64)
+        def tile(name, shape, dtype, tag=None):
+            return sb.tile(shape, dtype, name=name, tag=tag or name, align_bytes=64)
 
         def load_list(name, src):
             t = tile(name, [P, S // 16], U16)
             nc.sync.dma_start(t[:], src)
             return t
 
-        def load_scales(name, src, width, queue):
+        def load_scales(name, src, width):
             t = tile(name, [P, width], U8)
             nc.vector.memset(t[:].bitcast(I32), 0)
             for q in range(4):
-                queue.dma_start(t[32 * q : 32 * q + 4, :].bitcast(I32), src[0, 4 * q : 4 * q + 4, :].bitcast(I32))
+                nc.sync.dma_start(t[32 * q : 32 * q + 4, :].bitcast(I32), src[0, 4 * q : 4 * q + 4, :].bitcast(I32))
             return t
 
         def load_words(name, src):
@@ -52,118 +51,118 @@ def tile_picked_twlsoftbpagex_none_po_kernel(
             nc.sync.dma_start(t[:].bitcast(I32), src[0].bitcast(I32))
             return t
 
-        def deal(name, words, scales):
-            dw = tile(name + "_dw", [P, 2 * H], U8)
-            ds = tile(name + "_ds", [P, H], U8)
+        def deal_words(name, words, tag=None):
+            dw = tile(name, [P, 2 * H], U8, tag)
             nc.vector.tensor_copy(dw[:].rearrange("p (t m b) -> p t m b", t=PACK, b=2),
                                   words[:].rearrange("p (m t b) -> p t m b", t=PACK, b=2))
+            return dw
+
+        def deal_scales(name, scales, tag=None):
+            ds = tile(name, [P, H], U8, tag)
             nc.vector.tensor_copy(ds[:].rearrange("p (t m) -> p t m", t=PACK),
                                   scales[:].rearrange("p (m t) -> p t m", t=PACK))
-            return dw, ds
+            return ds
 
-        def pick(name, xw, xs, lst):
-            gw = tile(name + "_w", [P, S], I32)
-            gs = tile(name + "_s", [P, S], U8)
+        def pick_words(name, xw, lst):
+            gw = tile(name, [P, S], I32)
             nc.vector.tensor_copy(gw[:].bitcast(U32), xw[:].bitcast(U32).indirect(lst[:]))
-            nc.vector.tensor_copy(gs[:], xs[:].indirect(lst[:]))
-            return gw, gs
+            return gw
 
-        def product(out, w, t, rw, rs):
-            dw, ds = w
+        def pick_scales(name, xs, lst):
+            gs = tile(name, [P, S], U8)
+            nc.vector.tensor_copy(gs[:], xs[:].indirect(lst[:]))
+            return gs
+
+        def product(out, dw, ds, t, rw, rs):
             nc.tensor.matmul_mx(out=out, lhsT=dw[:, 2 * P * t : 2 * P * (t + 1)].bitcast(FP4X4),
                                 lhsT_scale=ds[:, P * t : P * (t + 1)], rhs=rw.bitcast(FP8X4), rhs_scale=rs,
                                 start=True, stop=True)
 
-        l_two = load_list("l_two", two)
-        w2w = load_words("w2w", w2_words)
-        l_offs = load_list("l_offs", offs)
-        w2s = load_scales("w2s", w2_scales, H, nc.sync)
         xw = tile("xw", [P, T], I32)
-        nc.sync.dma_start(xw[:], x_words[0].rearrange("p c r -> p (c r)").bitcast(I32))
-        xs = load_scales("xs", x_scales, T, nc.sync)
-        w1w = load_words("w1w", w1_words)
-        w1s = load_scales("w1s", w1_scales, H, nc.sync)
         gain = tile("gain", [P, PACK], F32)
+        nc.gpsimd.dma_start(xw[:], x_words[0].rearrange("p c r -> p (c r)").bitcast(I32))
+        l_two = load_list("l_two", two)
+        l_offs = load_list("l_offs", offs)
+        w2w = load_words("w2w", w2_words)
+        w1w = load_words("w1w", w1_words)
+        xs = load_scales("xs", x_scales, T)
+        w2s = load_scales("w2s", w2_scales, H)
+        w1s = load_scales("w1s", w1_scales, H)
         nc.sync.dma_start(gain[:], gn.rearrange("(p t) o -> p (t o)", t=PACK))
         l_n2 = load_list("l_n2", n2)
         l_n1 = load_list("l_n1", n1)
         w3w = load_words("w3w", w3_words)
-        w3s = load_scales("w3s", w3_scales, N, nc.sync)
+        w3s = load_scales("w3s", w3_scales, N)
         l_n3 = load_list("l_n3", n3)
         mem_rows = mem.rearrange("(p t) c -> p t c", t=PACK)
         out_rows = out_0.rearrange("(p t) c -> p t c", t=PACK)
-        page = []
-        for t in range(PACK):
-            pg = tile(f"page{t}", [P, U], F32)
-            nc.sync.dma_start(pg[:], mem_rows[:, t, :])
-            page.append(pg)
+        page = [tile(f"page{t}", [P, U], F32) for t in range(PACK)]
+        page_order = [1, 2, 3, 0]
+        for t in page_order:
+            nc.sync.dma_start(page[t][:], mem_rows[:, t, :])
 
-        w2 = deal("w2", w2w, w2s)
-        w1 = deal("w1", w1w, w1s)
-        tw, ts = pick("two", xw, xs, l_two)
-        ow, osc = pick("offs", xw, xs, l_offs)
+        w2d = deal_words("w2d", w2w)
+        ts = pick_scales("two_s", xs, l_two)
+        w2e = deal_scales("w2e", w2s)
+        tw = pick_words("two_w", xw, l_two)
+        d_ps = [ps.tile([P, S], F32, name=f"d_ps{t}", tag=f"bank{t}") for t in range(PACK)]
+        y_ps = [ps.tile([P, S], F32, name=f"y_ps{t}") for t in range(PACK)]
+        for t in range(PACK):
+            product(d_ps[t][:], w2d, w2e, t, tw[:], ts[:])
+        w1d = deal_words("w1d", w1w)
+        osc = pick_scales("offs_s", xs, l_offs)
+        w1e = deal_scales("w1e", w1s)
+        ow = pick_words("offs_w", xw, l_offs)
+        for t in range(PACK):
+            product(y_ps[t][:], w1d, w1e, t, ow[:], osc[:])
 
-        d_ps = [ps.tile([P, S], F32, name=f"d_ps{t}") for t in range(PACK)]
-        y_ps = [ps.tile([P, 2, S], F32, name=f"y_ps{i}") for i in range(2)]
+        dwin = [tile(f"dwin{t}", [P, 2 * S], F32) for t in range(PACK)]
+        ywin = [tile(f"ywin{t}", [P, 2 * S], F32) for t in range(PACK)]
+        dg = tile("dg", [P, PACK, S], F32)
+        yg = tile("yg", [P, PACK, S], F32)
+        zf = tile("zf", [P, PACK, S], F32, "w3w")
         for t in range(PACK):
-            product(d_ps[t][:], w2, t, tw[:], ts[:])
+            nc.scalar.activation(dwin[t][:, S:], d_ps[t][:], ACT.Tanh)
+            nc.vector.tensor_scalar(dwin[t][:, :S], d_ps[t][:], gain[:, t : t + 1], None, ALU.mult)
         for t in range(PACK):
-            product(y_ps[t // 2][:, t % 2, :], w1, t, ow[:], osc[:])
+            nc.vector.tensor_scalar(ywin[t][:, :S], y_ps[t][:], gain[:, t : t + 1], None, ALU.mult)
+        for t in range(PACK):
+            nc.scalar.activation(dg[:, t, :], dwin[t][:].indirect(l_n2[:]), ACT.Copy)
+            nc.vector.tensor_tensor(ywin[t][:, S:], dg[:, t, :], dwin[t][:, S:], ALU.mult)
+        w3d = deal_words("w3d", w3w, "gain")
+        w3e = deal_scales("w3e", w3s, "dwin0")
+        for t in range(PACK):
+            nc.scalar.activation(yg[:, t, :], ywin[t][:].indirect(l_n1[:]), ACT.Copy)
+            nc.vector.tensor_tensor(zf[:, t, :], yg[:, t, :], ywin[t][:, S:], ALU.subtract)
+        z = tile("z", [P, S, PACK], BF16, "w3s")
+        nc.vector.tensor_copy(z[:], zf[:].rearrange("p t c -> p c t"))
+        zw = tile("zw", [P, S], I32)
+        zs = tile("zs", [P, S], U8)
+        nc.vector.quantize_mx(out=zw[:].bitcast(FP8X4), scales=zs[:], in_=z[:].rearrange("p c t -> p (c t)"))
+        h_ps = [ps.tile([P, S], F32, name=f"h_ps{t}", tag=f"bank{t}") for t in range(PACK)]
+        for t in range(PACK):
+            product(h_ps[t][:], w3d, w3e, t, zw[:], zs[:])
 
-        th = tile("th", [P, PACK, S], F32)
-        dwin, ywin = [], []
+        old = [tile(f"old{t}", [P, S], F32) for t in range(PACK)]
+        for t in page_order:
+            nc.scalar.activation(old[t][:], page[t][:].indirect(l_n3[:]), ACT.Copy)
+        new = []
         for t in range(PACK):
-            nc.scalar.activation(th[:, t, :], d_ps[t][:], ACT.Tanh)
-            dw = tile(f"dwin{t}", [P, S], F32)
-            nc.vector.tensor_scalar(dw[:], d_ps[t][:], gain[:, t : t + 1], None, ALU.mult)
-            dwin.append(dw)
-        for t in range(PACK):
-            yw = tile(f"ywin{t}", [P, S], F32)
-            nc.vector.tensor_scalar(yw[:], y_ps[t // 2][:, t % 2, :], gain[:, t : t + 1], None, ALU.mult)
-            ywin.append(yw)
-        w3 = deal("w3", w3w, w3s)
-
-        h_ps = []
-        for a in range(2):
-            cols = slice(a * HALF // 16, (a + 1) * HALF // 16)
-            dg = tile(f"dg{a}", [P, PACK, HALF], F32)
-            yg = tile(f"yg{a}", [P, PACK, HALF], F32)
-            for t in range(PACK):
-                nc.scalar.activation(dg[:, t, :], dwin[t][:].indirect(l_n2[:, cols]), ACT.Copy)
-            for t in range(PACK):
-                nc.scalar.activation(yg[:, t, :], ywin[t][:].indirect(l_n1[:, cols]), ACT.Copy)
-            q = tile(f"q{a}", [P, PACK, HALF], F32)
-            nc.vector.tensor_tensor(q[:], dg[:], th[:, :, a * HALF : (a + 1) * HALF], ALU.mult)
-            z = tile(f"z{a}", [P, HALF * PACK], BF16)
-            nc.vector.tensor_tensor(z[:].rearrange("p (c i t) -> p c t i", i=4, t=PACK),
-                                    yg[:].rearrange("p t (c i) -> p c t i", i=4),
-                                    q[:].rearrange("p t (c i) -> p c t i", i=4), ALU.subtract)
-            zw = tile(f"zw{a}", [P, HALF], I32)
-            zs = tile(f"zs{a}", [P, HALF], U8)
-            nc.vector.quantize_mx(out=zw[:].bitcast(FP8X4), scales=zs[:], in_=z[:])
-            hp = ps.tile([P, PACK, HALF], F32, name=f"h_ps{a}")
-            for t in range(PACK):
-                product(hp[:, t, :], w3, t, zw[:], zs[:])
-            h_ps.append(hp)
-
-        old = tile("old", [P, PACK, S], F32)
-        for t in range(PACK):
-            nc.scalar.activation(old[:, t, :], page[t][:].indirect(l_n3[:]), ACT.Copy)
-        new = tile("new", [P, PACK, S], F32)
-        for a in range(2):
-            cols = slice(a * HALF, (a + 1) * HALF)
-            nc.vector.scalar_tensor_tensor(new[:, :, cols], old[:, :, cols], 0.5, h_ps[a][:], ALU.mult, ALU.max)
+            nw = tile(f"new{t}", [P, S], F32, f"old{t - 1}" if t else None)
+            nc.vector.scalar_tensor_tensor(nw[:], old[t][:], 0.5, h_ps[t][:], ALU.mult, ALU.max)
+            new.append(nw)
 
         rounded = [tile(f"rounded{c}", [P, CW, PACK], BF16) for c in range(CHUNKS)]
         codes = [tile(f"codes{c}", [P, CW], I32) for c in range(CHUNKS)]
         plane = tile("plane", [P, U], U8)
         words_out = out_1[0].rearrange("p c r -> p (c r)").bitcast(I32)
         for t in range(PACK):
-            nc.scalar.activation(page[t][:].indirect(l_n3[:]), new[:, t, :], ACT.Copy)
+            nc.scalar.activation(page[t][:].indirect(l_n3[:]), new[t][:], ACT.Copy)
             nc.sync.dma_start(out_rows[:, t, :], page[t][:])
-            for c in range(CHUNKS):
-                cols = slice(c * CW, (c + 1) * CW)
-                nc.vector.tensor_copy(rounded[c][:, :, t], page[t][:, cols])
+            for c in range(CHUNKS if t < 2 else CHUNKS - 1):
+                nc.vector.tensor_copy(rounded[c][:, :, t], page[t][:, c * CW : (c + 1) * CW])
+        for t in (2, 3):
+            nc.scalar.copy(rounded[CHUNKS - 1][:, :, t], page[t][:, U - CW :])
         for c in range(CHUNKS):
             cols = slice(c * CW, (c + 1) * CW)
             nc.vector.quantize_mx(out=codes[c][:].bitcast(FP8X4), scales=plane[:, cols],

@@ -39,16 +39,16 @@ def tile_picked_twlsoftbpagex_none_po_kernel(
             nc.sync.dma_start(t[:], src)
             return t
 
-        def load_scales(name, src, width):
+        def load_scales(name, src, width, queue=nc.sync):
             t = tile(name, [P, width], U8)
             nc.vector.memset(t[:].bitcast(I32), 0)
             for q in range(4):
-                nc.sync.dma_start(t[32 * q : 32 * q + 4, :].bitcast(I32), src[0, 4 * q : 4 * q + 4, :].bitcast(I32))
+                queue.dma_start(t[32 * q : 32 * q + 4, :].bitcast(I32), src[0, 4 * q : 4 * q + 4, :].bitcast(I32))
             return t
 
-        def load_words(name, src):
+        def load_words(name, src, queue=nc.sync):
             t = tile(name, [P, 2 * H], U8)
-            nc.sync.dma_start(t[:].bitcast(I32), src[0].bitcast(I32))
+            queue.dma_start(t[:].bitcast(I32), src[0].bitcast(I32))
             return t
 
         def deal_words(name, words, tag=None):
@@ -78,28 +78,32 @@ def tile_picked_twlsoftbpagex_none_po_kernel(
                                 lhsT_scale=ds[:, P * t : P * (t + 1)], rhs=rw.bitcast(FP8X4), rhs_scale=rs,
                                 start=True, stop=True)
 
-        xw = tile("xw", [P, T], I32)
-        gain = tile("gain", [P, PACK], F32)
-        nc.gpsimd.dma_start(xw[:], x_words[0].rearrange("p c r -> p (c r)").bitcast(I32))
-        l_two = load_list("l_two", two)
-        l_offs = load_list("l_offs", offs)
-        w2w = load_words("w2w", w2_words)
-        w1w = load_words("w1w", w1_words)
-        xs = load_scales("xs", x_scales, T)
-        w2s = load_scales("w2s", w2_scales, H)
-        w1s = load_scales("w1s", w1_scales, H)
-        nc.sync.dma_start(gain[:], gn.rearrange("(p t) o -> p (t o)", t=PACK))
-        l_n2 = load_list("l_n2", n2)
-        l_n1 = load_list("l_n1", n1)
-        w3w = load_words("w3w", w3_words)
-        w3s = load_scales("w3s", w3_scales, N)
-        l_n3 = load_list("l_n3", n3)
         mem_rows = mem.rearrange("(p t) c -> p t c", t=PACK)
         out_rows = out_0.rearrange("(p t) c -> p t c", t=PACK)
         page = [tile(f"page{t}", [P, U], F32) for t in range(PACK)]
-        page_order = [1, 2, 3, 0]
-        for t in page_order:
+        put_order = [2, 0, 1, 3]
+        page_order = put_order[1:] + put_order[:1]
+        xw = tile("xw", [P, T], I32)
+        gain = tile("gain", [P, PACK], F32)
+        nc.gpsimd.dma_start(gain[:], gn.rearrange("(p t) o -> p (t o)", t=PACK))
+        l_two = load_list("l_two", two)
+        w2w = load_words("w2w", w2_words)
+        xs = load_scales("xs", x_scales, T)
+        nc.sync.dma_start(xw[:], x_words[0].rearrange("p c r -> p (c r)").bitcast(I32))
+        w2s = load_scales("w2s", w2_scales, H)
+        l_offs = load_list("l_offs", offs)
+        w1w = load_words("w1w", w1_words)
+        l_n2 = load_list("l_n2", n2)
+        w1s = load_scales("w1s", w1_scales, H)
+        l_n1 = load_list("l_n1", n1)
+        for t in page_order[:2]:
             nc.sync.dma_start(page[t][:], mem_rows[:, t, :])
+        w3w = load_words("w3w", w3_words)
+        w3s = load_scales("w3s", w3_scales, N)
+        l_n3 = load_list("l_n3", n3)
+        for t in page_order[2:]:
+            nc.sync.dma_start(page[t][:], mem_rows[:, t, :])
+
 
         w2d = deal_words("w2d", w2w)
         ts = pick_scales("two_s", xs, l_two)
@@ -109,10 +113,10 @@ def tile_picked_twlsoftbpagex_none_po_kernel(
         y_ps = [ps.tile([P, S], F32, name=f"y_ps{t}") for t in range(PACK)]
         for t in range(PACK):
             product(d_ps[t][:], w2d, w2e, t, tw[:], ts[:])
-        w1d = deal_words("w1d", w1w)
         osc = pick_scales("offs_s", xs, l_offs)
-        w1e = deal_scales("w1e", w1s)
         ow = pick_words("offs_w", xw, l_offs)
+        w1d = deal_words("w1d", w1w, "xw")
+        w1e = deal_scales("w1e", w1s, "w2e")
         for t in range(PACK):
             product(y_ps[t][:], w1d, w1e, t, ow[:], osc[:])
 
@@ -120,7 +124,9 @@ def tile_picked_twlsoftbpagex_none_po_kernel(
         ywin = [tile(f"ywin{t}", [P, 2 * S], F32) for t in range(PACK)]
         dg = tile("dg", [P, PACK, S], F32)
         yg = tile("yg", [P, PACK, S], F32)
-        zf = tile("zf", [P, PACK, S], F32, "w3w")
+        prod = tile("prod", [P, PACK, S], F32, "w1s")
+        for t in range(PACK):
+            nc.vector.memset(ywin[t][:, S:], 0.0)
         for t in range(PACK):
             nc.scalar.activation(dwin[t][:, S:], d_ps[t][:], ACT.Tanh)
             nc.vector.tensor_scalar(dwin[t][:, :S], d_ps[t][:], gain[:, t : t + 1], None, ALU.mult)
@@ -128,41 +134,51 @@ def tile_picked_twlsoftbpagex_none_po_kernel(
             nc.vector.tensor_scalar(ywin[t][:, :S], y_ps[t][:], gain[:, t : t + 1], None, ALU.mult)
         for t in range(PACK):
             nc.scalar.activation(dg[:, t, :], dwin[t][:].indirect(l_n2[:]), ACT.Copy)
-            nc.vector.tensor_tensor(ywin[t][:, S:], dg[:, t, :], dwin[t][:, S:], ALU.mult)
+            nc.vector.tensor_tensor(prod[:, t, :], dg[:, t, :], dwin[t][:, S:], ALU.mult)
         w3d = deal_words("w3d", w3w, "gain")
-        w3e = deal_scales("w3e", w3s, "dwin0")
+        w3e = deal_scales("w3e", w3s, "w3w")
         for t in range(PACK):
             nc.scalar.activation(yg[:, t, :], ywin[t][:].indirect(l_n1[:]), ACT.Copy)
-            nc.vector.tensor_tensor(zf[:, t, :], yg[:, t, :], ywin[t][:, S:], ALU.subtract)
         z = tile("z", [P, S, PACK], BF16, "w3s")
-        nc.vector.tensor_copy(z[:], zf[:].rearrange("p t c -> p c t"))
+        nc.vector.tensor_tensor(z[:].rearrange("p (c i) t -> p c t i", i=4),
+                                yg[:].rearrange("p t (c i) -> p c t i", i=4),
+                                prod[:].rearrange("p t (c i) -> p c t i", i=4), ALU.subtract)
         zw = tile("zw", [P, S], I32)
         zs = tile("zs", [P, S], U8)
         nc.vector.quantize_mx(out=zw[:].bitcast(FP8X4), scales=zs[:], in_=z[:].rearrange("p c t -> p (c t)"))
         h_ps = [ps.tile([P, S], F32, name=f"h_ps{t}", tag=f"bank{t}") for t in range(PACK)]
-        for t in range(PACK):
+        for t in put_order:
             product(h_ps[t][:], w3d, w3e, t, zw[:], zs[:])
 
-        old = [tile(f"old{t}", [P, S], F32) for t in range(PACK)]
+        old_tags = dict(zip(page_order, ["ywin1", "ywin2", "ywin3", "old_last"]))
+        old = {}
         for t in page_order:
+            old[t] = tile(f"old{t}", [P, S], F32, old_tags[t])
             nc.scalar.activation(old[t][:], page[t][:].indirect(l_n3[:]), ACT.Copy)
-        new = []
-        for t in range(PACK):
-            nw = tile(f"new{t}", [P, S], F32, f"old{t - 1}" if t else None)
-            nc.vector.scalar_tensor_tensor(nw[:], old[t][:], 0.5, h_ps[t][:], ALU.mult, ALU.max)
-            new.append(nw)
+        new_tags = dict(zip(put_order, ["new_first", old_tags[put_order[0]], old_tags[put_order[1]], "new_first"]))
+        new = {}
+
+        def larger(t):
+            new[t] = tile(f"new{t}", [P, S], F32, new_tags[t])
+            nc.vector.scalar_tensor_tensor(new[t][:], old[t][:], 0.5, h_ps[t][:], ALU.mult, ALU.max)
+
+        for t in put_order[:-1]:
+            larger(t)
 
         rounded = [tile(f"rounded{c}", [P, CW, PACK], BF16) for c in range(CHUNKS)]
         codes = [tile(f"codes{c}", [P, CW], I32) for c in range(CHUNKS)]
         plane = tile("plane", [P, U], U8)
         words_out = out_1[0].rearrange("p c r -> p (c r)").bitcast(I32)
-        for t in range(PACK):
+        for t in put_order:
             nc.scalar.activation(page[t][:].indirect(l_n3[:]), new[t][:], ACT.Copy)
             nc.sync.dma_start(out_rows[:, t, :], page[t][:])
-            for c in range(CHUNKS if t < 2 else CHUNKS - 1):
-                nc.vector.tensor_copy(rounded[c][:, :, t], page[t][:, c * CW : (c + 1) * CW])
-        for t in (2, 3):
-            nc.scalar.copy(rounded[CHUNKS - 1][:, :, t], page[t][:, U - CW :])
+            for c in reversed(range(CHUNKS)) if t == put_order[0] else range(CHUNKS):
+                if t == put_order[-1] and c >= CHUNKS // 2:
+                    nc.scalar.copy(rounded[c][:, :, t], page[t][:, c * CW : (c + 1) * CW])
+                else:
+                    nc.vector.tensor_copy(rounded[c][:, :, t], page[t][:, c * CW : (c + 1) * CW])
+            if t == put_order[0]:
+                larger(put_order[-1])
         for c in range(CHUNKS):
             cols = slice(c * CW, (c + 1) * CW)
             nc.vector.quantize_mx(out=codes[c][:].bitcast(FP8X4), scales=plane[:, cols],

@@ -18,8 +18,7 @@ ACT = mybir.ActivationFunctionType
 
 P = 128
 PACK = 4
-CHUNKS = 4
-CW = U // CHUNKS
+CHUNKS = [slice(0, U // 2), slice(U // 2, 3 * U // 4), slice(3 * U // 4, U)]
 
 
 def tile_picked_twlsoftbpagex_none_po_kernel(
@@ -165,22 +164,22 @@ def tile_picked_twlsoftbpagex_none_po_kernel(
         for t in put_order[:-1]:
             larger(t)
 
-        rounded = [tile(f"rounded{c}", [P, CW, PACK], BF16) for c in range(CHUNKS)]
-        codes = [tile(f"codes{c}", [P, CW], I32) for c in range(CHUNKS)]
+        widths = [cols.stop - cols.start for cols in CHUNKS]
+        rounded = [tile(f"rounded{c}", [P, w, PACK], BF16) for c, w in enumerate(widths)]
+        codes = [tile(f"codes{c}", [P, w], I32) for c, w in enumerate(widths)]
         plane = tile("plane", [P, U], U8)
         words_out = out_1[0].rearrange("p c r -> p (c r)").bitcast(I32)
         for t in put_order:
             nc.scalar.activation(page[t][:].indirect(l_n3[:]), new[t][:], ACT.Copy)
             nc.sync.dma_start(out_rows[:, t, :], page[t][:])
-            for c in reversed(range(CHUNKS)) if t == put_order[0] else range(CHUNKS):
-                if t == put_order[-1] and c >= CHUNKS // 2:
-                    nc.scalar.copy(rounded[c][:, :, t], page[t][:, c * CW : (c + 1) * CW])
+            for c in (1, 2, 0) if t == put_order[0] else (0, 1, 2):
+                if t == put_order[-1] and c > 0:
+                    nc.scalar.copy(rounded[c][:, :, t], page[t][:, CHUNKS[c]])
                 else:
-                    nc.vector.tensor_copy(rounded[c][:, :, t], page[t][:, c * CW : (c + 1) * CW])
+                    nc.vector.tensor_copy(rounded[c][:, :, t], page[t][:, CHUNKS[c]])
             if t == put_order[0]:
                 larger(put_order[-1])
-        for c in range(CHUNKS):
-            cols = slice(c * CW, (c + 1) * CW)
+        for c, cols in enumerate(CHUNKS):
             nc.vector.quantize_mx(out=codes[c][:].bitcast(FP8X4), scales=plane[:, cols],
                                   in_=rounded[c][:].rearrange("p c t -> p (c t)"))
             nc.sync.dma_start(words_out[:, cols], codes[c][:])

from contextlib import ExitStack

import concourse.mybir as mybir

K, T, S, N, H, U = 512, 2048, 256, 512, 512, 1024
FLOPS = 3 * 2 * 512 * 512 * 256

F32 = mybir.dt.float32
BF16 = mybir.dt.bfloat16
I32 = mybir.dt.int32
U32 = mybir.dt.uint32
U16 = mybir.dt.uint16
U8 = mybir.dt.uint8
FP8X4 = mybir.dt.float8_e4m3fn_x4
FP4X4 = mybir.dt.float4_e2m1fn_x4
ALU = mybir.AluOpType
ACT = mybir.ActivationFunctionType

P = 128
PACK = 4
CHUNKS = [slice(0, U // 2), slice(U // 2, 3 * U // 4), slice(3 * U // 4, U)]


def tile_picked_twlsoftbpagex_none_po_kernel(
    tc, x_words, x_scales, w1_words, w1_scales, w2_words, w2_scales, gn, w3_words, w3_scales, mem,
    offs, two, n1, n2, n3, out_0, out_1, out_2,
):
    nc = tc.nc
    with ExitStack() as ctx:
        sb = ctx.enter_context(tc.tile_pool(name="sb", bufs=1))
        ps = ctx.enter_context(tc.psum_pool(name="ps", bufs=1))

        def tile(name, shape, dtype, tag=None):
            return sb.tile(shape, dtype, name=name, tag=tag or name, align_bytes=64)

        def load_list(name, src):
            t = tile(name, [P, S // 16], U16)
            nc.sync.dma_start(t[:], src)
            return t

        def load_scales(name, src, width, queue=nc.sync):
            t = tile(name, [P, width], U8)
            nc.vector.memset(t[:].bitcast(I32), 0)
            for q in range(4):
                queue.dma_start(t[32 * q : 32 * q + 4, :].bitcast(I32), src[0, 4 * q : 4 * q + 4, :].bitcast(I32))
            return t

        def load_words(name, src, queue=nc.sync):
            t = tile(name, [P, 2 * H], U8)
            queue.dma_start(t[:].bitcast(I32), src[0].bitcast(I32))
            return t

        def deal_words(name, words, tag=None):
            dw = tile(name, [P, 2 * H], U8, tag)
            nc.vector.tensor_copy(dw[:].rearrange("p (t m b) -> p t m b", t=PACK, b=2),
                                  words[:].rearrange("p (m t b) -> p t m b", t=PACK, b=2))
            return dw

        def deal_scales(name, scales, tag=None):
            ds = tile(name, [P, H], U8, tag)
            nc.vector.tensor_copy(ds[:].rearrange("p (t m) -> p t m", t=PACK),
                                  scales[:].rearrange("p (m t) -> p t m", t=PACK))
            return ds

        def pick_words(name, xw, lst):
            gw = tile(name, [P, S], I32)
            nc.vector.tensor_copy(gw[:].bitcast(U32), xw[:].bitcast(U32).indirect(lst[:]))
            return gw

        def pick_scales(name, xs, lst):
            gs = tile(name, [P, S], U8)
            nc.vector.tensor_copy(gs[:], xs[:].indirect(lst[:]))
            return gs

        def product(out, dw, ds, t, rw, rs):
            nc.tensor.matmul_mx(out=out, lhsT=dw[:, 2 * P * t : 2 * P * (t + 1)].bitcast(FP4X4),
                                lhsT_scale=ds[:, P * t : P * (t + 1)], rhs=rw.bitcast(FP8X4), rhs_scale=rs,
                                start=True, stop=True)

        mem_rows = mem.rearrange("(p t) c -> p t c", t=PACK)
        out_rows = out_0.rearrange("(p t) c -> p t c", t=PACK)
        page = [tile(f"page{t}", [P, U], F32) for t in range(PACK)]
        put_order = [2, 0, 1, 3]
        page_order = put_order[1:] + put_order[:1]
        xw = tile("xw", [P, T], I32)
        gain = tile("gain", [P, PACK], F32)
        nc.gpsimd.dma_start(gain[:], gn.rearrange("(p t) o -> p (t o)", t=PACK))
        l_two = load_list("l_two", two)
        w2w = load_words("w2w", w2_words)
        xs = load_scales("xs", x_scales, T)
        nc.sync.dma_start(xw[:], x_words[0].rearrange("p c r -> p (c r)").bitcast(I32))
        w2s = load_scales("w2s", w2_scales, H)
        l_offs = load_list("l_offs", offs)
        w1w = load_words("w1w", w1_words)
        l_n2 = load_list("l_n2", n2)
        w1s = load_scales("w1s", w1_scales, H)
        l_n1 = load_list("l_n1", n1)
        for t in page_order[:2]:
            nc.sync.dma_start(page[t][:], mem_rows[:, t, :])
        w3w = load_words("w3w", w3_words)
        w3s = load_scales("w3s", w3_scales, N)
        l_n3 = load_list("l_n3", n3)
        for t in page_order[2:]:
            nc.sync.dma_start(page[t][:], mem_rows[:, t, :])


        w2d = deal_words("w2d", w2w)
        ts = pick_scales("two_s", xs, l_two)
        w2e = deal_scales("w2e", w2s)
        tw = pick_words("two_w", xw, l_two)
        d_ps = [ps.tile([P, S], F32, name=f"d_ps{t}", tag=f"bank{t}") for t in range(PACK)]
        y_ps = [ps.tile([P, S], F32, name=f"y_ps{t}") for t in range(PACK)]
        for t in range(PACK):
            product(d_ps[t][:], w2d, w2e, t, tw[:], ts[:])
        osc = pick_scales("offs_s", xs, l_offs)
        ow = pick_words("offs_w", xw, l_offs)
        w1d = deal_words("w1d", w1w, "xw")
        w1e = deal_scales("w1e", w1s, "w2e")
        for t in range(PACK):
            product(y_ps[t][:], w1d, w1e, t, ow[:], osc[:])

        dwin = [tile(f"dwin{t}", [P, 2 * S], F32) for t in range(PACK)]
        ywin = [tile(f"ywin{t}", [P, 2 * S], F32) for t in range(PACK)]
        dg = tile("dg", [P, PACK, S], F32)
        yg = tile("yg", [P, PACK, S], F32)
        prod = tile("prod", [P, PACK, S], F32, "w1s")
        for t in range(PACK):
            nc.vector.memset(ywin[t][:, S:], 0.0)
        for t in range(PACK):
            nc.scalar.activation(dwin[t][:, S:], d_ps[t][:], ACT.Tanh)
            nc.vector.tensor_scalar(dwin[t][:, :S], d_ps[t][:], gain[:, t : t + 1], None, ALU.mult)
        for t in range(PACK):
            nc.vector.tensor_scalar(ywin[t][:, :S], y_ps[t][:], gain[:, t : t + 1], None, ALU.mult)
        for t in range(PACK):
            nc.scalar.activation(dg[:, t, :], dwin[t][:].indirect(l_n2[:]), ACT.Copy)
            nc.vector.tensor_tensor(prod[:, t, :], dg[:, t, :], dwin[t][:, S:], ALU.mult)
        w3d = deal_words("w3d", w3w, "gain")
        w3e = deal_scales("w3e", w3s, "w3w")
        for t in range(PACK):
            nc.scalar.activation(yg[:, t, :], ywin[t][:].indirect(l_n1[:]), ACT.Copy)
        z = tile("z", [P, S, PACK], BF16, "w3s")
        nc.vector.tensor_tensor(z[:].rearrange("p (c i) t -> p c t i", i=4),
                                yg[:].rearrange("p t (c i) -> p c t i", i=4),
                                prod[:].rearrange("p t (c i) -> p c t i", i=4), ALU.subtract)
        zw = tile("zw", [P, S], I32)
        zs = tile("zs", [P, S], U8)
        nc.vector.quantize_mx(out=zw[:].bitcast(FP8X4), scales=zs[:], in_=z[:].rearrange("p c t -> p (c t)"))
        h_ps = [ps.tile([P, S], F32, name=f"h_ps{t}", tag=f"bank{t}") for t in range(PACK)]
        for t in put_order:
            product(h_ps[t][:], w3d, w3e, t, zw[:], zs[:])

        old_tags = dict(zip(page_order, ["ywin1", "ywin2", "ywin3", "old_last"]))
        old = {}
        for t in page_order:
            old[t] = tile(f"old{t}", [P, S], F32, old_tags[t])
            nc.scalar.activation(old[t][:], page[t][:].indirect(l_n3[:]), ACT.Copy)
        new_tags = dict(zip(put_order, ["new_first", old_tags[put_order[0]], old_tags[put_order[1]], "new_first"]))
        new = {}

        def larger(t):
            new[t] = tile(f"new{t}", [P, S], F32, new_tags[t])
            nc.vector.scalar_tensor_tensor(new[t][:], old[t][:], 0.5, h_ps[t][:], ALU.mult, ALU.max)

        for t in put_order[:-1]:
            larger(t)

        widths = [cols.stop - cols.start for cols in CHUNKS]
        rounded = [tile(f"rounded{c}", [P, w, PACK], BF16) for c, w in enumerate(widths)]
        codes = [tile(f"codes{c}", [P, w], I32) for c, w in enumerate(widths)]
        plane = tile("plane", [P, U], U8)
        words_out = out_1[0].rearrange("p c r -> p (c r)").bitcast(I32)
        for t in put_order:
            nc.scalar.activation(page[t][:].indirect(l_n3[:]), new[t][:], ACT.Copy)
            nc.sync.dma_start(out_rows[:, t, :], page[t][:])
            for c in (1, 2, 0) if t == put_order[0] else (0, 1, 2):
                if t == put_order[-1] and c > 0:
                    nc.scalar.copy(rounded[c][:, :, t], page[t][:, CHUNKS[c]])
                else:
                    nc.vector.tensor_copy(rounded[c][:, :, t], page[t][:, CHUNKS[c]])
            if t == put_order[0]:
                larger(put_order[-1])
        for c, cols in enumerate(CHUNKS):
            nc.vector.quantize_mx(out=codes[c][:].bitcast(FP8X4), scales=plane[:, cols],
                                  in_=rounded[c][:].rearrange("p c t -> p (c t)"))
            nc.sync.dma_start(words_out[:, cols], codes[c][:])
        for q in range(4):
            queue = nc.scalar if q % 2 else nc.sync
            queue.dma_start(out_2[0, 4 * q : 4 * q + 4, :].bitcast(I32), plane[32 * q : 32 * q + 4, :].bitcast(I32))
